import numpy as np
import ml_dtypes


def mxq(x, axis, fmt="e4m3"):
    dtype, down = {"e4m3": (ml_dtypes.float8_e4m3fn, 7), "e5m2": (ml_dtypes.float8_e5m2, 14)}[fmt]
    v = np.moveaxis(np.asarray(x, np.float32).astype(ml_dtypes.bfloat16).astype(np.float64), axis, -1)
    blocks = v.reshape(v.shape[:-1] + (-1, 32))
    amax = np.abs(blocks).max(-1, keepdims=True)
    byte = np.maximum(np.where(amax > 0, np.frexp(amax)[1] - 1 + 127, 0) - down, 1)
    scale = np.exp2(byte - 127.0)
    codes = (blocks / scale).astype(np.float32).astype(dtype).astype(np.float64)
    return np.moveaxis((codes * scale).reshape(v.shape), -1, axis)


WIDE = False


def mx_kscale(k):
    if not WIDE:
        return np.ones(k)
    levels = np.array([10, -10, 5, -5, 0])
    if k % 512:
        return np.exp2(np.random.permutation(np.resize(levels, k // 32))).repeat(32)
    a = np.empty((k // 512, 16))
    for p in range(k // 512):
        a[p, :8] = np.random.permutation(np.resize(levels, 8))
        for g in range(8):
            far = levels[np.abs(levels - a[p, g]) >= 10]
            a[p, g + 8] = far[np.random.randint(len(far))]
    return np.exp2(a.ravel()).repeat(32)


def f64(x):
    return np.asarray(x).astype(np.float64)


def striped(idx):
    return np.tile(idx.reshape(-1, 16).T, (8, 1)).astype(np.uint16)


def unstriped(offs):
    return offs[:16].T.reshape(-1).astype(np.int64)


E2M1 = np.array([0.0, 0.5, 1.0, 1.5, 2.0, 3.0, 4.0, 6.0, -0.0, -0.5, -1.0, -1.5, -2.0, -3.0, -4.0, -6.0])


def pack_weight(w, fmt):
    k, n = w.shape
    w = f64(np.asarray(w, np.float32).astype(ml_dtypes.bfloat16)).reshape(k // 32, 32, n)
    amax = np.abs(w).max(1)
    if fmt == "e4m3":
        byte = np.frexp(amax)[1] - 1 + 127 - 7
    else:
        mant, ex = np.frexp(amax / 6.0)
        byte = np.where(mant > 0.5, ex, ex - 1) + 127
    byte = np.clip(np.where(amax > 0, byte, 1), 1, 254)
    scaled = (w * np.exp2(127.0 - byte)[:, None, :]).reshape(k, n).astype(np.float32)
    by_word = np.ascontiguousarray(scaled.reshape(k // 512, 128, 4, n).transpose(0, 1, 3, 2))
    if fmt == "e4m3":
        words = by_word.astype(ml_dtypes.float8_e4m3fn).view(np.uint8)
    else:
        c = by_word.astype(ml_dtypes.float4_e2m1fn).view(np.uint8) & 0xF
        words = (c[..., 0::2] | (c[..., 1::2] << 4)).reshape(k // 512, 128, 2 * n)
    return np.ascontiguousarray(words), np.ascontiguousarray(byte.astype(np.uint8).reshape(k // 512, 16, n))


def unpack_weight(words, scales, fmt):
    g, _, n = scales.shape
    words = np.ascontiguousarray(words).reshape(g, 128, n, -1)
    if fmt == "e4m3":
        vals = words.view(ml_dtypes.float8_e4m3fn).astype(np.float64)
    else:
        nib = np.empty((g, 128, n, 4), np.uint8)
        nib[..., 0::2] = words & 0xF
        nib[..., 1::2] = words >> 4
        vals = E2M1[nib]
    vals = vals * np.repeat(np.exp2(scales.astype(np.float64) - 127.0), 8, axis=1)[..., None]
    return vals.transpose(0, 1, 3, 2).reshape(g * 512, n)


def gelu(v):
    return 0.5 * v * (1.0 + np.tanh(np.sqrt(2.0 / np.pi) * (v + 0.044715 * v**3)))


def often(T, S):
    return np.random.permutation(T)[(T * np.random.uniform(0, 1, S) ** 4).astype(np.int64)]


K, M, H, N, T, S, P = 1024, 512, 1024, 512, 2048, 1024, 512


def setup_inputs():
    n = np.random.standard_normal
    s = mx_kscale(K)[:, None]
    s2 = mx_kscale(M)[:, None]
    u = mx_kscale(H)[:, None]
    d = {}
    d["tab_words"], d["tab_scales"] = pack_weight(n((K, T)) * s, "e4m3")
    d["tab2_words"], d["tab2_scales"] = pack_weight(n((M, T)) * s2, "e4m3")
    d["tab3_words"], d["tab3_scales"] = pack_weight(n((M, T)) * s2, "e4m3")
    d["offs"] = striped(np.random.permutation(T)[:S])
    d["offs2"] = striped(np.random.permutation(T)[:S])
    d["offs3"] = striped(np.random.permutation(T)[:S])
    d["pos1"] = striped(np.random.permutation(S)[:P])
    d["pos2"] = striped(often(S, P))
    d["pos3"] = striped(often(S, P))
    d["w1"] = (1.4 * n((K, H)) / K ** 0.5 / s).astype(np.float32)
    d["w2_words"], d["w2_scales"] = pack_weight(1.6 * n((M, H)) / M ** 0.5 / s2 * u.T, "e2m1")
    d["w3"] = (0.6 * n((M, H)) / M ** 0.5 / s2 * u.T).astype(np.float32)
    d["w4_words"], d["w4_scales"] = pack_weight(1.3 * n((H, N)) / H ** 0.5 / u, "e4m3")
    d["gain"] = np.exp(0.4 * n(N)).astype(np.float32)
    return d


def reference(tab_words, tab_scales, tab2_words, tab2_scales, tab3_words, tab3_scales, offs, offs2, offs3,
              pos1, pos2, pos3, w1, w2_words, w2_scales, w3, w4_words, w4_scales, gain):
    v = unpack_weight(tab_words, tab_scales, "e4m3")[:, unstriped(offs)]
    v2 = unpack_weight(tab2_words, tab2_scales, "e4m3")[:, unstriped(offs2)]
    v3 = unpack_weight(tab3_words, tab3_scales, "e4m3")[:, unstriped(offs3)]
    w2 = unpack_weight(w2_words, w2_scales, "e2m1")
    w4 = unpack_weight(w4_words, w4_scales, "e4m3")
    a = mxq(f64(w1), 0, "e4m3").T @ v
    b = w2.T @ v2
    d = mxq(f64(w3), 0, "e4m3").T @ v3
    x = a[:, unstriped(pos1)]
    bend = x / (1.0 + x * x)
    z = mxq(bend * b[:, unstriped(pos2)] + d[:, unstriped(pos3)], 0, "e4m3")
    return (w4.T @ z) * f64(gain)[:, None]

@@ -1,0 +1,295 @@
+from contextlib import ExitStack
+
+import concourse.mybir as mybir
+
+K, M, H, N, T, S, PK = 1024, 512, 1024, 512, 2048, 1024, 512
+FLOPS = 2 * (K * H * S + 2 * M * H * S + H * N * PK)
+
+F32 = mybir.dt.float32
+BF16 = mybir.dt.bfloat16
+I32 = mybir.dt.int32
+U32 = mybir.dt.uint32
+U16 = mybir.dt.uint16
+U8 = mybir.dt.uint8
+FP8X4 = mybir.dt.float8_e4m3fn_x4
+FP4X4 = mybir.dt.float4_e2m1fn_x4
+ACT = mybir.ActivationFunctionType
+ALU = mybir.AluOpType
+
+P = 128
+BANK = 512
+
+
+def tile_list_algae_harvest_join_kernel(
+    tc, tab_words, tab_scales, tab2_words, tab2_scales, tab3_words, tab3_scales, offs, offs2, offs3,
+    pos1, pos2, pos3, w1, w2_words, w2_scales, w3, w4_words, w4_scales, gain, out,
+):
+    nc = tc.nc
+    with ExitStack() as ctx:
+        keep = ctx.enter_context(tc.tile_pool(name="keep", bufs=1))
+        work = ctx.enter_context(tc.tile_pool(name="work", bufs=1))
+        psum = ctx.enter_context(tc.psum_pool(name="psum", bufs=1))
+
+        def zeroed_plane(name, width):
+            plane = keep.tile([P, width], U8, name=name, align_bytes=64)
+            nc.vector.memset(plane[:].bitcast(I32), 0)
+            return plane
+
+        def load_plane(plane, scales, eng):
+            passes = scales.shape[0]
+            for q in range(4):
+                eng.dma_start(
+                    out=plane[32 * q : 32 * q + 4 * passes, :].bitcast(I32),
+                    in_=scales[:, 4 * q : 4 * q + 4, :].bitcast(I32),
+                )
+
+        def load_list(name, src):
+            tile = keep.tile(list(src.shape), U16, name=name)
+            nc.sync.dma_start(tile[:], src)
+            return tile
+
+        def load_words(name, words):
+            tile = keep.tile([P, words.shape[1]], I32, name=name, align_bytes=64)
+            nc.sync.dma_start(out=tile[:], in_=words.rearrange("p c i -> p (c i)").bitcast(I32))
+            return tile
+
+        def load_weight(w, a, b):
+            raw = work.tile([P, 4, BANK], F32, name="raw", tag="raw", bufs=6, align_bytes=64)
+            nc.sync.dma_start(
+                out=raw[:],
+                in_=w[512 * a : 512 * (a + 1), 512 * b : 512 * (b + 1)].rearrange("(p j) c -> p j c", j=4),
+            )
+            return raw
+
+        w2_plane_raw = zeroed_plane("w2_plane_raw", H)
+        tab2_plane = zeroed_plane("tab2_plane", T)
+        tab_plane = zeroed_plane("tab_plane", T)
+        tab3_plane = zeroed_plane("tab3_plane", T)
+        w4_plane = zeroed_plane("w4_plane", N)
+        warm = keep.tile([P, 2], F32, name="warm")
+        nc.vector.memset(warm[:, 0:1], 1.0)
+        nc.scalar.activation(warm[:, 1:2], warm[:, 0:1], ACT.Abs_reciprocal_sqrt)
+
+        w1_raw, w3_raw, tab_tiles = {}, {}, {}
+        w2_raw = keep.tile([P, 2 * H], U8, name="w2_raw", align_bytes=64)
+        nc.sync.dma_start(out=w2_raw[:].bitcast(I32), in_=w2_words[0].bitcast(I32))
+        tab2_tile = load_words("tab2_tile", tab2_words[0])
+        load_plane(w2_plane_raw, w2_scales, nc.sync)
+        list2 = load_list("list2", offs2)
+        w1_raw[(0, 0)] = load_weight(w1, 0, 0)
+        load_plane(tab2_plane, tab2_scales, nc.sync)
+        tab_tiles[0] = load_words("tab_tile0", tab_words[0])
+        list1 = load_list("list1", offs)
+        load_plane(tab_plane, tab_scales, nc.sync)
+        w1_raw[(1, 0)] = load_weight(w1, 1, 0)
+        tab_tiles[1] = load_words("tab_tile1", tab_words[1])
+        list3 = load_list("list3", offs3)
+        tab3_tile = load_words("tab3_tile", tab3_words[0])
+        load_plane(tab3_plane, tab3_scales, nc.sync)
+        w3_raw[0] = load_weight(w3, 0, 0)
+        pick1 = load_list("pick1", pos1)
+        pick2 = load_list("pick2", pos2)
+        pick3 = load_list("pick3", pos3)
+        w1_raw[(0, 1)] = load_weight(w1, 0, 1)
+        w1_raw[(1, 1)] = load_weight(w1, 1, 1)
+        w3_raw[1] = load_weight(w3, 0, 1)
+        w4_tiles = [load_words("w4_tile%d" % a, w4_words[a]) for a in range(2)]
+        load_plane(w4_plane, w4_scales, nc.sync)
+        gain_tile = keep.tile([P, N // P], F32, name="gain_tile")
+        with nc.allow_non_contiguous_dma(reason="one gain a partition"):
+            nc.sync.dma_start(out=gain_tile[:], in_=gain.rearrange("(c p) -> p c", p=P))
+
+        def gather_words(name, table, offsets):
+            picked = keep.tile([P, S], I32, name=name, align_bytes=64)
+            nc.vector.tensor_copy(picked[:].bitcast(U32), table[:].bitcast(U32).indirect(offsets[:]))
+            return picked
+
+        def gather_plane(name, plane, offsets):
+            picked = keep.tile([P, S], U8, name=name, align_bytes=64)
+            nc.vector.tensor_copy(picked[:], plane[:].indirect(offsets[:]))
+            return picked
+
+        def round_weight(raw, eng):
+            rounded = work.tile([P, 4 * BANK], BF16, name="rounded", tag="rounded", bufs=3, align_bytes=64)
+            dst = rounded[:].rearrange("p (t m j) -> p m j t", t=4, j=4)
+            src = raw[:].rearrange("p j (m t) -> p m j t", t=4)
+            if eng == "s":
+                nc.scalar.copy(dst, src)
+            elif eng == "v":
+                nc.vector.tensor_copy(dst, src)
+            else:
+                nc.gpsimd.tensor_scalar(dst, src, 1.0, 0.0, ALU.mult, ALU.add)
+            return rounded
+
+        def quantise(name, rounded):
+            codes = keep.tile([P, BANK], U32, name=name + "_codes", align_bytes=64)
+            plane = keep.tile([P, BANK], U8, name=name + "_plane", align_bytes=64)
+            nc.vector.quantize_mx(out=codes[:].bitcast(FP8X4), scales=plane[:], in_=rounded[:])
+            return codes, plane
+
+        def product(tag, bufs, passes):
+            rows = work.tile([P, S], F32, name=tag, tag=tag, bufs=bufs)
+            for h in range(S // BANK):
+                cols = slice(BANK * h, BANK * (h + 1))
+                acc = psum.tile([P, BANK], F32, name="acc", tag="acc", bufs=4)
+                for i, (lhs, lhs_plane, rhs, rhs_plane, first) in enumerate(passes):
+                    nc.tensor.matmul_mx(
+                        out=acc[:], lhsT=lhs, lhsT_scale=lhs_plane,
+                        rhs=rhs[:, cols].bitcast(FP8X4), rhs_scale=rhs_plane[first:P, cols],
+                        start=(i == 0), stop=(i == len(passes) - 1),
+                    )
+                nc.scalar.copy(rows[:, cols], acc[:])
+            return rows
+
+        w2_codes = keep.tile([P, 2 * H], U8, name="w2_codes", align_bytes=64)
+        nc.vector.tensor_copy(
+            w2_codes[:].rearrange("p (b t m e) -> p b m t e", b=2, t=4, e=2),
+            w2_raw[:].rearrange("p (b m t e) -> p b m t e", b=2, t=4, e=2),
+        )
+        w2_plane = keep.tile([P, H], U8, name="w2_plane", align_bytes=64)
+        nc.vector.tensor_copy(
+            w2_plane[:].rearrange("p (b t m) -> p b m t", b=2, t=4),
+            w2_plane_raw[:].rearrange("p (b m t) -> p b m t", b=2, t=4),
+        )
+        v2 = gather_words("v2", tab2_tile, list2)
+        v2_plane = gather_plane("v2_plane", tab2_plane, list2)
+
+        E = "ssssvv"
+        w1_q = {}
+        w3_q = {}
+
+        def b_rows(s):
+            return product("b_rows", 8, [(
+                w2_codes[:, 2 * P * s : 2 * P * (s + 1)].bitcast(FP4X4), w2_plane[:, P * s : P * (s + 1)],
+                v2, v2_plane, 0)])
+
+        def a_rows(s):
+            b, t = divmod(s, 4)
+            cols = slice(P * t, P * (t + 1))
+            return product("a_rows", 3, [
+                (w1_q[(a, b)][0][:, cols].bitcast(FP8X4), w1_q[(a, b)][1][:, cols], v[a], v_plane, 4 * a)
+                for a in range(2)])
+
+        def d_rows(s):
+            b, t = divmod(s, 4)
+            cols = slice(P * t, P * (t + 1))
+            return product("d_rows", 3, [
+                (w3_q[b][0][:, cols].bitcast(FP8X4), w3_q[b][1][:, cols], v3, v3_plane, 0)])
+
+        r00 = round_weight(w1_raw[(0, 0)], E[0])
+        r10 = round_weight(w1_raw[(1, 0)], E[1])
+        v = [gather_words("v0", tab_tiles[0], list1)]
+        w1_q[(0, 0)] = quantise("w1_00", r00)
+        v_plane = gather_plane("v_plane", tab_plane, list1)
+        bs = [b_rows(s) for s in range(8)]
+        v.append(gather_words("v1", tab_tiles[1], list1))
+        w1_q[(1, 0)] = quantise("w1_10", r10)
+        r3 = round_weight(w3_raw[0], E[2])
+        a_tiles = {0: a_rows(0), 1: a_rows(1)}
+        v3 = gather_words("v3", tab3_tile, list3)
+        w3_q[0] = quantise("w3_0", r3)
+        v3_plane = gather_plane("v3_plane", tab3_plane, list3)
+
+        xs, rs, z_tiles, ds = {}, {}, {}, {}
+        HALF = PK // 2
+
+        def curve(s):
+            x = work.tile([P, PK], F32, name="x", tag="x", bufs=3)
+            nc.vector.tensor_copy(x[:], a_tiles[s][:].indirect(pick1[:]))
+            r = work.tile([P, PK], F32, name="r", tag="r", bufs=3)
+            nc.scalar.activation(r[:], x[:], ACT.Square)
+            nc.scalar.activation(r[:], r[:], ACT.Abs_reciprocal_sqrt, bias=1.0)
+            nc.scalar.activation(r[:], r[:], ACT.Square)
+            xs[s], rs[s] = x, r
+
+        def join(s, pieces):
+            b, t = divmod(s, 4)
+            if t == 0:
+                z_tiles[b] = work.tile([P, 4, PK], F32, name="raw", tag="raw", bufs=6, align_bytes=64)
+            xb = work.tile([P, PK], F32, name="xb", tag="xb", bufs=2)
+            u = work.tile([P, PK], F32, name="u", tag="u", bufs=2)
+            nc.vector.tensor_tensor(xb[:], bs[s][:].indirect(pick2[:]), xs[s][:], ALU.mult)
+            nc.vector.tensor_tensor(u[:], xb[:], rs[s][:], ALU.mult)
+            width = PK // pieces
+            for h in range(pieces):
+                cols = slice(width * h, width * (h + 1))
+                nc.vector.tensor_tensor(
+                    z_tiles[b][:, t, cols], ds[s][:].indirect(pick3[:, width // 16 * h : width // 16 * (h + 1)]),
+                    u[:, cols], ALU.add)
+
+        def round_z(b, cols, copy):
+            width = cols.stop - cols.start
+            rounded = work.tile([P, 4 * width], BF16, name="rounded", tag="rounded", bufs=3, align_bytes=64)
+            copy(
+                rounded[:].rearrange("p (c i t) -> p c t i", i=4, t=4),
+                z_tiles[b][:, :, cols].rearrange("p t (c i) -> p c t i", i=4),
+            )
+            return rounded
+
+        def quantise_z(name, rounded):
+            width = rounded.shape[1] // 4
+            codes = keep.tile([P, width], U32, name=name + "_codes", align_bytes=64)
+            plane = keep.tile([P, width], U8, name=name + "_plane", align_bytes=64)
+            nc.vector.quantize_mx(out=codes[:].bitcast(FP8X4), scales=plane[:], in_=rounded[:])
+            return codes, plane
+
+        def final_pass(acc, b, c, codes, plane):
+            cols = slice(P * c, P * (c + 1))
+            nc.tensor.matmul_mx(
+                out=acc, lhsT=w4_tiles[b][:, cols].bitcast(FP8X4), lhsT_scale=w4_plane[4 * b : P, cols],
+                rhs=codes.bitcast(FP8X4), rhs_scale=plane, start=(b == 0), stop=(b == 1),
+            )
+
+        def store(h, accs):
+            result = work.tile([P, N // P, HALF], F32, name="result", tag="result", bufs=2)
+            for c in range(N // P):
+                if h == 0 or c < 2:
+                    nc.scalar.activation(result[:, c, :], accs[c], ACT.Copy, scale=gain_tile[:, c : c + 1])
+                else:
+                    nc.vector.tensor_scalar(result[:, c, :], accs[c], gain_tile[:, c : c + 1], None, ALU.mult)
+                if c % 2 == 1:
+                    nc.sync.dma_start(
+                        out=out[P * (c - 1) : P * (c + 1), HALF * h : HALF * (h + 1)].rearrange("(c p) j -> p c j", p=P),
+                        in_=result[:, c - 1 : c + 1, :])
+
+        late = [psum.tile([P, HALF], F32, name="late%d" % c) for c in range(N // P)]
+        curve(0)
+        ds[0] = d_rows(0)
+        for s in range(8):
+            if len(bs) < 8:
+                bs.append(b_rows(len(bs)))
+            if s == 0:
+                ra = round_weight(w1_raw[(0, 1)], E[3])
+            if s == 1:
+                w1_q[(0, 1)] = quantise("w1_01", ra)
+                rb = round_weight(w1_raw[(1, 1)], E[4])
+            if s == 2:
+                w1_q[(1, 1)] = quantise("w1_11", rb)
+                rc = round_weight(w3_raw[1], E[5])
+            if s == 3:
+                w3_q[1] = quantise("w3_1", rc)
+            if s + 2 < 8:
+                a_tiles[s + 2] = a_rows(s + 2)
+            if s + 1 < 8:
+                curve(s + 1)
+                ds[s + 1] = d_rows(s + 1)
+            join(s, 2 if s == 7 else 1)
+            if s == 4:
+                z0 = quantise_z("z0", round_z(0, slice(0, PK), nc.scalar.copy))
+                for c in range(N // P):
+                    final_pass(late[c][:], 0, c, z0[0][:, HALF:], z0[1][:, HALF:])
+        rounded_early = round_z(1, slice(0, HALF), nc.scalar.copy)
+        rounded_late = round_z(1, slice(HALF, PK), nc.vector.tensor_copy)
+        z_early = quantise_z("z1e", rounded_early)
+        z_late = quantise_z("z1l", rounded_late)
+        early = []
+        for c in range(N // P):
+            acc = psum.tile([P, BANK], F32, name="acc", tag="acc", bufs=4)
+            final_pass(acc[:, :HALF], 0, c, z0[0][:, :HALF], z0[1][:, :HALF])
+            early.append(acc[:, :HALF])
+        for c in range(N // P):
+            final_pass(early[c], 1, c, z_early[0][:], z_early[1][:])
+        for c in range(N // P):
+            final_pass(late[c][:], 1, c, z_late[0][:], z_late[1][:])
+        store(0, early)
+        store(1, [acc[:] for acc in late])

@@ -73,11 +73,11 @@ def tile_list_algae_harvest_join_kernel(
         w1_raw, w3_raw, tab_tiles = {}, {}, {}
         w2_raw = keep.tile([P, 2 * H], U8, name="w2_raw", align_bytes=64)
         nc.sync.dma_start(out=w2_raw[:].bitcast(I32), in_=w2_words[0].bitcast(I32))
-        tab2_tile = load_words("tab2_tile", tab2_words[0])
-        load_plane(w2_plane_raw, w2_scales, nc.sync)
         list2 = load_list("list2", offs2)
-        w1_raw[(0, 0)] = load_weight(w1, 0, 0)
         load_plane(tab2_plane, tab2_scales, nc.sync)
+        tab2_tile = load_words("tab2_tile", tab2_words[0])
+        w1_raw[(0, 0)] = load_weight(w1, 0, 0)
+        load_plane(w2_plane_raw, w2_scales, nc.sync)
         tab_tiles[0] = load_words("tab_tile0", tab_words[0])
         list1 = load_list("list1", offs)
         load_plane(tab_plane, tab_scales, nc.sync)
@@ -154,7 +154,7 @@ def tile_list_algae_harvest_join_kernel(
         v2 = gather_words("v2", tab2_tile, list2)
         v2_plane = gather_plane("v2_plane", tab2_plane, list2)
 
-        E = "ssssvv"
+        E = "gggggg"
         w1_q = {}
         w3_q = {}
 

@@ -49,7 +49,10 @@ def tile_list_algae_harvest_join_kernel(
             return tile
 
         def load_words(name, words):
-            tile = keep.tile([P, words.shape[1]], I32, name=name, align_bytes=64)
+            if words.shape[1] == T:
+                tile = work.tile([P, T], I32, name=name, tag="table", bufs=4, align_bytes=64)
+            else:
+                tile = keep.tile([P, words.shape[1]], I32, name=name, align_bytes=64)
             nc.sync.dma_start(out=tile[:], in_=words.rearrange("p c i -> p (c i)").bitcast(I32))
             return tile
 
@@ -76,21 +79,21 @@ def tile_list_algae_harvest_join_kernel(
         list2 = load_list("list2", offs2)
         load_plane(tab2_plane, tab2_scales, nc.sync)
         tab2_tile = load_words("tab2_tile", tab2_words[0])
-        w1_raw[(0, 0)] = load_weight(w1, 0, 0)
         load_plane(w2_plane_raw, w2_scales, nc.sync)
         tab_tiles[0] = load_words("tab_tile0", tab_words[0])
         list1 = load_list("list1", offs)
         load_plane(tab_plane, tab_scales, nc.sync)
-        w1_raw[(1, 0)] = load_weight(w1, 1, 0)
+        w1_raw[(0, 0)] = load_weight(w1, 0, 0)
         tab_tiles[1] = load_words("tab_tile1", tab_words[1])
+        w1_raw[(1, 0)] = load_weight(w1, 1, 0)
         list3 = load_list("list3", offs3)
-        tab3_tile = load_words("tab3_tile", tab3_words[0])
         load_plane(tab3_plane, tab3_scales, nc.sync)
-        w3_raw[0] = load_weight(w3, 0, 0)
+        tab3_tile = load_words("tab3_tile", tab3_words[0])
         pick1 = load_list("pick1", pos1)
+        w3_raw[0] = load_weight(w3, 0, 0)
+        w1_raw[(0, 1)] = load_weight(w1, 0, 1)
         pick2 = load_list("pick2", pos2)
         pick3 = load_list("pick3", pos3)
-        w1_raw[(0, 1)] = load_weight(w1, 0, 1)
         w1_raw[(1, 1)] = load_weight(w1, 1, 1)
         w3_raw[1] = load_weight(w3, 0, 1)
         w4_tiles = [load_words("w4_tile%d" % a, w4_words[a]) for a in range(2)]
@@ -111,14 +114,15 @@ def tile_list_algae_harvest_join_kernel(
 
         def round_weight(raw, eng):
             rounded = work.tile([P, 4 * BANK], BF16, name="rounded", tag="rounded", bufs=3, align_bytes=64)
-            dst = rounded[:].rearrange("p (t m j) -> p m j t", t=4, j=4)
-            src = raw[:].rearrange("p j (m t) -> p m j t", t=4)
+            dst = rounded[:].rearrange("p (t m j) -> p m t j", t=4, j=4)
+            src = raw[:].rearrange("p j (m t) -> p m t j", t=4)
             if eng == "s":
                 nc.scalar.copy(dst, src)
             elif eng == "v":
                 nc.vector.tensor_copy(dst, src)
             else:
-                nc.gpsimd.tensor_scalar(dst, src, 1.0, 0.0, ALU.mult, ALU.add)
+                for m in range(0, P, 128):
+                    nc.gpsimd.tensor_scalar(dst[:, m : m + 128], src[:, m : m + 128], 1.0, 0.0, ALU.mult, ALU.add)
             return rounded
 
         def quantise(name, rounded):
@@ -128,7 +132,7 @@ def tile_list_algae_harvest_join_kernel(
             return codes, plane
 
         def product(tag, bufs, passes):
-            rows = work.tile([P, S], F32, name=tag, tag=tag, bufs=bufs)
+            rows = work.tile([P, S], F32, name=tag, tag=tag, bufs=bufs, align_bytes=64)
             for h in range(S // BANK):
                 cols = slice(BANK * h, BANK * (h + 1))
                 acc = psum.tile([P, BANK], F32, name="acc", tag="acc", bufs=4)
@@ -143,8 +147,8 @@ def tile_list_algae_harvest_join_kernel(
 
         w2_codes = keep.tile([P, 2 * H], U8, name="w2_codes", align_bytes=64)
         nc.vector.tensor_copy(
-            w2_codes[:].rearrange("p (b t m e) -> p b m t e", b=2, t=4, e=2),
-            w2_raw[:].rearrange("p (b m t e) -> p b m t e", b=2, t=4, e=2),
+            w2_codes[:].bitcast(U16).rearrange("p (b t m) -> p b m t", b=2, t=4),
+            w2_raw[:].bitcast(U16).rearrange("p (b m t) -> p b m t", b=2, t=4),
         )
         w2_plane = keep.tile([P, H], U8, name="w2_plane", align_bytes=64)
         nc.vector.tensor_copy(
@@ -154,7 +158,7 @@ def tile_list_algae_harvest_join_kernel(
         v2 = gather_words("v2", tab2_tile, list2)
         v2_plane = gather_plane("v2_plane", tab2_plane, list2)
 
-        E = "gggggg"
+        E = "gggggs"
         w1_q = {}
         w3_q = {}
 
@@ -166,60 +170,56 @@ def tile_list_algae_harvest_join_kernel(
         def a_rows(s):
             b, t = divmod(s, 4)
             cols = slice(P * t, P * (t + 1))
-            return product("a_rows", 3, [
+            return product("a_rows", 4, [
                 (w1_q[(a, b)][0][:, cols].bitcast(FP8X4), w1_q[(a, b)][1][:, cols], v[a], v_plane, 4 * a)
                 for a in range(2)])
 
         def d_rows(s):
             b, t = divmod(s, 4)
             cols = slice(P * t, P * (t + 1))
-            return product("d_rows", 3, [
+            return product("table", 4, [
                 (w3_q[b][0][:, cols].bitcast(FP8X4), w3_q[b][1][:, cols], v3, v3_plane, 0)])
 
-        r00 = round_weight(w1_raw[(0, 0)], E[0])
-        r10 = round_weight(w1_raw[(1, 0)], E[1])
-        v = [gather_words("v0", tab_tiles[0], list1)]
-        w1_q[(0, 0)] = quantise("w1_00", r00)
-        v_plane = gather_plane("v_plane", tab_plane, list1)
-        bs = [b_rows(s) for s in range(8)]
-        v.append(gather_words("v1", tab_tiles[1], list1))
-        w1_q[(1, 0)] = quantise("w1_10", r10)
-        r3 = round_weight(w3_raw[0], E[2])
-        a_tiles = {0: a_rows(0), 1: a_rows(1)}
-        v3 = gather_words("v3", tab3_tile, list3)
-        w3_q[0] = quantise("w3_0", r3)
-        v3_plane = gather_plane("v3_plane", tab3_plane, list3)
-
-        xs, rs, z_tiles, ds = {}, {}, {}, {}
+        xs, rs, z_tiles, ds, ts, us = {}, {}, {}, {}, {}, {}
         HALF = PK // 2
+        AHEAD = 4
+        units = [(s, 0, PK) for s in range(7)] + [(7, 0, HALF), (7, HALF, HALF + HALF // 2), (7, HALF + HALF // 2, PK)]
 
-        def curve(s):
-            x = work.tile([P, PK], F32, name="x", tag="x", bufs=3)
-            nc.vector.tensor_copy(x[:], a_tiles[s][:].indirect(pick1[:]))
-            r = work.tile([P, PK], F32, name="r", tag="r", bufs=3)
+        def tmp(name, bufs, i):
+            return work.tile([P, units[i][2] - units[i][1]], F32, name=name, tag=name, bufs=bufs, align_bytes=64)
+
+        def offsets(pick, i):
+            return pick[:, units[i][1] // 16 : units[i][2] // 16]
+
+        def curve(i):
+            x = tmp("x", AHEAD, i) if i < AHEAD or True else tmp("b_rows", 8, i)
+            nc.vector.tensor_copy(x[:], a_tiles[units[i][0]][:].indirect(offsets(pick1, i)))
+            r = tmp("r", 4, i)
             nc.scalar.activation(r[:], x[:], ACT.Square)
             nc.scalar.activation(r[:], r[:], ACT.Abs_reciprocal_sqrt, bias=1.0)
             nc.scalar.activation(r[:], r[:], ACT.Square)
-            xs[s], rs[s] = x, r
+            xs[i], rs[i] = x, r
 
-        def join(s, pieces):
+        def bend(i):
+            eng = nc.gpsimd if i < 0 else nc.vector
+            ts[i] = tmp("bend", 2, i)
+            eng.tensor_tensor(ts[i][:], bs[units[i][0]][:].indirect(offsets(pick2, i)), xs[i][:], ALU.mult)
+
+        def scale(i):
+            us[i] = tmp("u", 2, i)
+            nc.vector.tensor_tensor(us[i][:], ts[i][:], rs[i][:], ALU.mult)
+
+        def shift(i):
+            s, lo, hi = units[i]
             b, t = divmod(s, 4)
             if t == 0:
                 z_tiles[b] = work.tile([P, 4, PK], F32, name="raw", tag="raw", bufs=6, align_bytes=64)
-            xb = work.tile([P, PK], F32, name="xb", tag="xb", bufs=2)
-            u = work.tile([P, PK], F32, name="u", tag="u", bufs=2)
-            nc.vector.tensor_tensor(xb[:], bs[s][:].indirect(pick2[:]), xs[s][:], ALU.mult)
-            nc.vector.tensor_tensor(u[:], xb[:], rs[s][:], ALU.mult)
-            width = PK // pieces
-            for h in range(pieces):
-                cols = slice(width * h, width * (h + 1))
-                nc.vector.tensor_tensor(
-                    z_tiles[b][:, t, cols], ds[s][:].indirect(pick3[:, width // 16 * h : width // 16 * (h + 1)]),
-                    u[:, cols], ALU.add)
+            nc.vector.tensor_tensor(
+                z_tiles[b][:, t, lo:hi], ds[s][:].indirect(offsets(pick3, i)), us[i][:], ALU.add)
 
         def round_z(b, cols, copy):
             width = cols.stop - cols.start
-            rounded = work.tile([P, 4 * width], BF16, name="rounded", tag="rounded", bufs=3, align_bytes=64)
+            rounded = work.tile([P, 4 * width], BF16, name="z_rounded", tag="z_rounded", bufs=2, align_bytes=64)
             copy(
                 rounded[:].rearrange("p (c i t) -> p c t i", i=4, t=4),
                 z_tiles[b][:, :, cols].rearrange("p t (c i) -> p c t i", i=4),
@@ -240,56 +240,72 @@ def tile_list_algae_harvest_join_kernel(
                 rhs=codes.bitcast(FP8X4), rhs_scale=plane, start=(b == 0), stop=(b == 1),
             )
 
-        def store(h, accs):
-            result = work.tile([P, N // P, HALF], F32, name="result", tag="result", bufs=2)
+        def store(cols, accs, on_scalar):
+            result = work.tile([P, N // P, cols.stop - cols.start], F32, name="raw", tag="raw", bufs=6, align_bytes=64)
             for c in range(N // P):
-                if h == 0 or c < 2:
+                if c < on_scalar:
                     nc.scalar.activation(result[:, c, :], accs[c], ACT.Copy, scale=gain_tile[:, c : c + 1])
                 else:
                     nc.vector.tensor_scalar(result[:, c, :], accs[c], gain_tile[:, c : c + 1], None, ALU.mult)
                 if c % 2 == 1:
                     nc.sync.dma_start(
-                        out=out[P * (c - 1) : P * (c + 1), HALF * h : HALF * (h + 1)].rearrange("(c p) j -> p c j", p=P),
+                        out=out[P * (c - 1) : P * (c + 1), cols].rearrange("(c p) j -> p c j", p=P),
                         in_=result[:, c - 1 : c + 1, :])
 
-        late = [psum.tile([P, HALF], F32, name="late%d" % c) for c in range(N // P)]
-        curve(0)
-        ds[0] = d_rows(0)
-        for s in range(8):
-            if len(bs) < 8:
-                bs.append(b_rows(len(bs)))
-            if s == 0:
-                ra = round_weight(w1_raw[(0, 1)], E[3])
-            if s == 1:
+        def finish(i, copy, tag, on_scalar):
+            cols = slice(units[i][1], units[i][2])
+            accs = []
+            for c in range(N // P):
+                acc = psum.tile([P, BANK], F32, name=tag, tag=tag, bufs=4)
+                accs.append(acc[:, : cols.stop - cols.start])
+                final_pass(accs[c], 0, c, z0[0][:, cols], z0[1][:, cols])
+            codes, plane = quantise_z("z1_%d" % i, round_z(1, cols, copy))
+            for c in range(N // P):
+                final_pass(accs[c], 1, c, codes[:], plane[:])
+            store(cols, accs, on_scalar)
+
+        r00 = round_weight(w1_raw[(0, 0)], E[0])
+        r10 = round_weight(w1_raw[(1, 0)], E[1])
+        bs = [b_rows(s) for s in range(8)]
+        v = [gather_words("v0", tab_tiles[0], list1)]
+        v_plane = gather_plane("v_plane", tab_plane, list1)
+        w1_q[(0, 0)] = quantise("w1_00", r00)
+        v.append(gather_words("v1", tab_tiles[1], list1))
+        w1_q[(1, 0)] = quantise("w1_10", r10)
+        r3 = round_weight(w3_raw[0], E[2])
+        a_tiles = {s: a_rows(s) for s in range(AHEAD)}
+        v3 = gather_words("v3", tab3_tile, list3)
+        for i in range(2):
+            curve(i)
+        v3_plane = gather_plane("v3_plane", tab3_plane, list3)
+        w3_q[0] = quantise("w3_0", r3)
+        ra = round_weight(w1_raw[(0, 1)], E[3])
+        rb = round_weight(w1_raw[(1, 1)], E[4])
+        rc = round_weight(w3_raw[1], E[5])
+        for i in range(2, AHEAD):
+            curve(i)
+        for i in range(2):
+            ds[i] = d_rows(i)
+        bend(0)
+        for i in range(len(units)):
+            if i == 0:
                 w1_q[(0, 1)] = quantise("w1_01", ra)
-                rb = round_weight(w1_raw[(1, 1)], E[4])
-            if s == 2:
+            if i == 0:
                 w1_q[(1, 1)] = quantise("w1_11", rb)
-                rc = round_weight(w3_raw[1], E[5])
-            if s == 3:
+            if i == 0:
                 w3_q[1] = quantise("w3_1", rc)
-            if s + 2 < 8:
-                a_tiles[s + 2] = a_rows(s + 2)
-            if s + 1 < 8:
-                curve(s + 1)
-                ds[s + 1] = d_rows(s + 1)
-            join(s, 2 if s == 7 else 1)
-            if s == 4:
+            if i + AHEAD < 8:
+                a_tiles[i + AHEAD] = a_rows(i + AHEAD)
+            if i + 2 < 8:
+                ds[i + 2] = d_rows(i + 2)
+            scale(i)
+            if i + AHEAD < len(units):
+                curve(i + AHEAD)
+            if i + 1 < len(units):
+                bend(i + 1)
+            shift(i)
+            if i == 5:
                 z0 = quantise_z("z0", round_z(0, slice(0, PK), nc.scalar.copy))
-                for c in range(N // P):
-                    final_pass(late[c][:], 0, c, z0[0][:, HALF:], z0[1][:, HALF:])
-        rounded_early = round_z(1, slice(0, HALF), nc.scalar.copy)
-        rounded_late = round_z(1, slice(HALF, PK), nc.vector.tensor_copy)
-        z_early = quantise_z("z1e", rounded_early)
-        z_late = quantise_z("z1l", rounded_late)
-        early = []
-        for c in range(N // P):
-            acc = psum.tile([P, BANK], F32, name="acc", tag="acc", bufs=4)
-            final_pass(acc[:, :HALF], 0, c, z0[0][:, :HALF], z0[1][:, :HALF])
-            early.append(acc[:, :HALF])
-        for c in range(N // P):
-            final_pass(early[c], 1, c, z_early[0][:], z_early[1][:])
-        for c in range(N // P):
-            final_pass(late[c][:], 1, c, z_late[0][:], z_late[1][:])
-        store(0, early)
-        store(1, [acc[:] for acc in late])
+        finish(7, nc.scalar.copy, "fin", 4)
+        finish(8, nc.vector.tensor_copy, "acc", 4)
+        finish(9, nc.vector.tensor_copy, "fin", 2)

@@ -2,8 +2,8 @@ from contextlib import ExitStack
 
 import concourse.mybir as mybir
 
-K, M, H, N, T, S, PK = 1024, 512, 1024, 512, 2048, 1024, 512
-FLOPS = 2 * (K * H * S + 2 * M * H * S + H * N * PK)
+K, M, H, N, T, S, PICKS = 1024, 512, 1024, 512, 2048, 1024, 512
+FLOPS = 2 * (K * H * S + 2 * M * H * S + H * N * PICKS)
 
 F32 = mybir.dt.float32
 BF16 = mybir.dt.bfloat16
@@ -17,7 +17,19 @@ ACT = mybir.ActivationFunctionType
 ALU = mybir.AluOpType
 
 P = 128
+PACK = 4
+PASS = P * PACK
 BANK = 512
+BANKS = 8
+SLICES = H // P
+LAST = SLICES - 1
+OUT_TILES = N // P
+PER_COLUMN = 16
+ALL_PICKS = slice(0, PICKS)
+
+PIECES = [slice(0, PICKS // 2), slice(PICKS // 2, 3 * PICKS // 4), slice(3 * PICKS // 4, PICKS)]
+W1_LAST_AFTER = 1
+Z0_AFTER = 6
 
 
 def tile_list_algae_harvest_join_kernel(
@@ -26,223 +38,193 @@ def tile_list_algae_harvest_join_kernel(
 ):
     nc = tc.nc
     with ExitStack() as ctx:
-        keep = ctx.enter_context(tc.tile_pool(name="keep", bufs=1))
-        work = ctx.enter_context(tc.tile_pool(name="work", bufs=1))
+        pool = ctx.enter_context(tc.tile_pool(name="sbuf", bufs=1))
         psum = ctx.enter_context(tc.psum_pool(name="psum", bufs=1))
 
+        def tile_of(tag, shape, dtype, bufs=1):
+            return pool.tile(shape, dtype, name=tag, tag=tag, bufs=bufs, align_bytes=64)
+
+        def big_tile(shape):
+            return tile_of("big", shape, F32, bufs=5)
+
+        def table_tile(width, dtype):
+            return tile_of("table", [P, width], dtype, bufs=PACK)
+
+        def rounded_tile(width):
+            return tile_of("rounded", [P, width], BF16, bufs=3)
+
+        def bank_tile():
+            return psum.tile([P, BANK], F32, name="bank", tag="bank", bufs=BANKS)
+
         def zeroed_plane(name, width):
-            plane = keep.tile([P, width], U8, name=name, align_bytes=64)
+            plane = tile_of(name, [P, width], U8)
             nc.vector.memset(plane[:].bitcast(I32), 0)
             return plane
 
-        def load_plane(plane, scales, eng):
+        def load_plane(plane, scales):
             passes = scales.shape[0]
-            for q in range(4):
-                eng.dma_start(
-                    out=plane[32 * q : 32 * q + 4 * passes, :].bitcast(I32),
-                    in_=scales[:, 4 * q : 4 * q + 4, :].bitcast(I32),
+            for quadrant in range(4):
+                nc.sync.dma_start(
+                    out=plane[32 * quadrant : 32 * quadrant + 4 * passes, :].bitcast(I32),
+                    in_=scales[:, 4 * quadrant : 4 * quadrant + 4, :].bitcast(I32),
                 )
 
         def load_list(name, src):
-            tile = keep.tile(list(src.shape), U16, name=name)
+            tile = pool.tile(list(src.shape), U16, name=name)
             nc.sync.dma_start(tile[:], src)
             return tile
 
-        def load_words(name, words):
-            if words.shape[1] == T:
-                tile = work.tile([P, T], I32, name=name, tag="table", bufs=4, align_bytes=64)
-            else:
-                tile = keep.tile([P, words.shape[1]], I32, name=name, align_bytes=64)
+        def load_words(tile, words):
             nc.sync.dma_start(out=tile[:], in_=words.rearrange("p c i -> p (c i)").bitcast(I32))
             return tile
 
-        def load_weight(w, a, b):
-            raw = work.tile([P, 4, BANK], F32, name="raw", tag="raw", bufs=6, align_bytes=64)
-            nc.sync.dma_start(
-                out=raw[:],
-                in_=w[512 * a : 512 * (a + 1), 512 * b : 512 * (b + 1)].rearrange("(p j) c -> p j c", j=4),
-            )
+        def load_weight(raw, w, g, half):
+            rows = w[PASS * g : PASS * (g + 1), PASS * half : PASS * (half + 1)]
+            nc.sync.dma_start(out=raw[:], in_=rows.rearrange("(p j) c -> p j c", j=PACK))
             return raw
 
-        w2_plane_raw = zeroed_plane("w2_plane_raw", H)
         tab2_plane = zeroed_plane("tab2_plane", T)
+        w2_plane_raw = zeroed_plane("w2_plane_raw", H)
         tab_plane = zeroed_plane("tab_plane", T)
         tab3_plane = zeroed_plane("tab3_plane", T)
         w4_plane = zeroed_plane("w4_plane", N)
-        warm = keep.tile([P, 2], F32, name="warm")
-        nc.vector.memset(warm[:, 0:1], 1.0)
-        nc.scalar.activation(warm[:, 1:2], warm[:, 0:1], ACT.Abs_reciprocal_sqrt)
 
-        w1_raw, w3_raw, tab_tiles = {}, {}, {}
-        w2_raw = keep.tile([P, 2 * H], U8, name="w2_raw", align_bytes=64)
+        block = [P, PACK, PASS]
+        w1_raw, w3_raw = {}, {}
+        w2_raw = tile_of("w2_raw", [P, 2 * H], U8)
         nc.sync.dma_start(out=w2_raw[:].bitcast(I32), in_=w2_words[0].bitcast(I32))
         list2 = load_list("list2", offs2)
-        load_plane(tab2_plane, tab2_scales, nc.sync)
-        tab2_tile = load_words("tab2_tile", tab2_words[0])
-        load_plane(w2_plane_raw, w2_scales, nc.sync)
-        tab_tiles[0] = load_words("tab_tile0", tab_words[0])
+        load_plane(tab2_plane, tab2_scales)
+        tab2_tile = load_words(table_tile(T, I32), tab2_words[0])
+        load_plane(w2_plane_raw, w2_scales)
+        tab_tile0 = load_words(table_tile(T, I32), tab_words[0])
         list1 = load_list("list1", offs)
-        load_plane(tab_plane, tab_scales, nc.sync)
-        w1_raw[(0, 0)] = load_weight(w1, 0, 0)
-        tab_tiles[1] = load_words("tab_tile1", tab_words[1])
-        w1_raw[(1, 0)] = load_weight(w1, 1, 0)
+        load_plane(tab_plane, tab_scales)
+        w1_raw[0, 0] = load_weight(big_tile(block), w1, 0, 0)
         list3 = load_list("list3", offs3)
-        load_plane(tab3_plane, tab3_scales, nc.sync)
-        tab3_tile = load_words("tab3_tile", tab3_words[0])
+        load_plane(tab3_plane, tab3_scales)
+        tab_tile1 = load_words(table_tile(T, I32), tab_words[1])
+        w1_raw[1, 0] = load_weight(tile_of("w1_shared", block, F32), w1, 1, 0)
+        tab3_tile = load_words(table_tile(T, I32), tab3_words[0])
         pick1 = load_list("pick1", pos1)
-        w3_raw[0] = load_weight(w3, 0, 0)
-        w1_raw[(0, 1)] = load_weight(w1, 0, 1)
+        w3_raw[0] = load_weight(big_tile(block), w3, 0, 0)
+        w1_raw[0, 1] = load_weight(big_tile(block), w1, 0, 1)
         pick2 = load_list("pick2", pos2)
         pick3 = load_list("pick3", pos3)
-        w1_raw[(1, 1)] = load_weight(w1, 1, 1)
-        w3_raw[1] = load_weight(w3, 0, 1)
-        w4_tiles = [load_words("w4_tile%d" % a, w4_words[a]) for a in range(2)]
-        load_plane(w4_plane, w4_scales, nc.sync)
-        gain_tile = keep.tile([P, N // P], F32, name="gain_tile")
-        with nc.allow_non_contiguous_dma(reason="one gain a partition"):
+        w1_raw[1, 1] = load_weight(big_tile(block), w1, 1, 1)
+        w3_raw[1] = load_weight(big_tile(block), w3, 0, 1)
+        w4_tiles = [load_words(tile_of("w4_tile%d" % g, [P, N], I32), w4_words[g]) for g in range(2)]
+        load_plane(w4_plane, w4_scales)
+        gain_tile = pool.tile([P, OUT_TILES], F32, name="gain_tile")
+        with nc.allow_non_contiguous_dma(reason="gain[128 c + p] goes to partition p, as the rows of out do"):
             nc.sync.dma_start(out=gain_tile[:], in_=gain.rearrange("(c p) -> p c", p=P))
 
         def gather_words(name, table, offsets):
-            picked = keep.tile([P, S], I32, name=name, align_bytes=64)
+            picked = tile_of(name, [P, S], I32)
             nc.vector.tensor_copy(picked[:].bitcast(U32), table[:].bitcast(U32).indirect(offsets[:]))
             return picked
 
         def gather_plane(name, plane, offsets):
-            picked = keep.tile([P, S], U8, name=name, align_bytes=64)
+            picked = tile_of(name, [P, S], U8)
             nc.vector.tensor_copy(picked[:], plane[:].indirect(offsets[:]))
             return picked
 
-        def round_weight(raw, eng):
-            rounded = work.tile([P, 4 * BANK], BF16, name="rounded", tag="rounded", bufs=3, align_bytes=64)
-            dst = rounded[:].rearrange("p (t m j) -> p m t j", t=4, j=4)
-            src = raw[:].rearrange("p j (m t) -> p m t j", t=4)
-            if eng == "s":
-                nc.scalar.copy(dst, src)
-            elif eng == "v":
-                nc.vector.tensor_copy(dst, src)
-            else:
-                for m in range(0, P, 128):
-                    nc.gpsimd.tensor_scalar(dst[:, m : m + 128], src[:, m : m + 128], 1.0, 0.0, ALU.mult, ALU.add)
-            return rounded
+        def dealt_views(rounded, raw):
+            return (
+                rounded.rearrange("p (t m j) -> p m t j", t=PACK, j=PACK),
+                raw[:].rearrange("p j (m t) -> p m t j", t=PACK),
+            )
 
-        def quantise(name, rounded):
-            codes = keep.tile([P, BANK], U32, name=name + "_codes", align_bytes=64)
-            plane = keep.tile([P, BANK], U8, name=name + "_plane", align_bytes=64)
+        def gpsimd_copy(dst, src):
+            nc.gpsimd.tensor_scalar(dst, src, 1.0, 0.0, ALU.mult, ALU.add)
+
+        def quantise(rounded, codes_tag, plane_tag):
+            width = rounded.shape[1] // PACK
+            codes = tile_of(codes_tag, [P, width], U32)
+            plane = tile_of(plane_tag, [P, width], U8)
             nc.vector.quantize_mx(out=codes[:].bitcast(FP8X4), scales=plane[:], in_=rounded[:])
-            return codes, plane
+            return codes[:], plane[:]
 
-        def product(tag, bufs, passes):
-            rows = work.tile([P, S], F32, name=tag, tag=tag, bufs=bufs, align_bytes=64)
-            for h in range(S // BANK):
-                cols = slice(BANK * h, BANK * (h + 1))
-                acc = psum.tile([P, BANK], F32, name="acc", tag="acc", bufs=4)
-                for i, (lhs, lhs_plane, rhs, rhs_plane, first) in enumerate(passes):
+        def product(rows, passes):
+            for first_col in range(0, S, BANK):
+                cols = slice(first_col, first_col + BANK)
+                acc = bank_tile()
+                for g, (lhs, lhs_plane, rhs, rhs_plane, first_row) in enumerate(passes):
                     nc.tensor.matmul_mx(
                         out=acc[:], lhsT=lhs, lhsT_scale=lhs_plane,
-                        rhs=rhs[:, cols].bitcast(FP8X4), rhs_scale=rhs_plane[first:P, cols],
-                        start=(i == 0), stop=(i == len(passes) - 1),
+                        rhs=rhs[:, cols].bitcast(FP8X4), rhs_scale=rhs_plane[first_row:P, cols],
+                        start=(g == 0), stop=(g == len(passes) - 1),
                     )
                 nc.scalar.copy(rows[:, cols], acc[:])
             return rows
 
-        w2_codes = keep.tile([P, 2 * H], U8, name="w2_codes", align_bytes=64)
-        nc.vector.tensor_copy(
-            w2_codes[:].bitcast(U16).rearrange("p (b t m) -> p b m t", b=2, t=4),
-            w2_raw[:].bitcast(U16).rearrange("p (b m t) -> p b m t", b=2, t=4),
-        )
-        w2_plane = keep.tile([P, H], U8, name="w2_plane", align_bytes=64)
-        nc.vector.tensor_copy(
-            w2_plane[:].rearrange("p (b t m) -> p b m t", b=2, t=4),
-            w2_plane_raw[:].rearrange("p (b m t) -> p b m t", b=2, t=4),
-        )
-        v2 = gather_words("v2", tab2_tile, list2)
-        v2_plane = gather_plane("v2_plane", tab2_plane, list2)
+        def lhs_of(quantised, s):
+            codes, plane = quantised
+            places = slice(P * (s % PACK), P * (s % PACK + 1))
+            return codes[:, places].bitcast(FP8X4), plane[:, places]
 
-        E = "gggggs"
-        w1_q = {}
-        w3_q = {}
+        def make_a(s):
+            rows = tile_of("a_rows%d" % (s % PACK), [P, S], F32)
+            return product(rows, [lhs_of(w1_q[g, s // PACK], s) + (v[g], v_plane, 4 * g) for g in range(2)])
 
-        def b_rows(s):
-            return product("b_rows", 8, [(
-                w2_codes[:, 2 * P * s : 2 * P * (s + 1)].bitcast(FP4X4), w2_plane[:, P * s : P * (s + 1)],
-                v2, v2_plane, 0)])
+        def make_b(s, rows):
+            lhs = w2_codes[:, 2 * P * s : 2 * P * (s + 1)].bitcast(FP4X4)
+            return product(rows, [(lhs, w2_plane[:, P * s : P * (s + 1)], v2, v2_plane, 0)])
 
-        def a_rows(s):
-            b, t = divmod(s, 4)
-            cols = slice(P * t, P * (t + 1))
-            return product("a_rows", 4, [
-                (w1_q[(a, b)][0][:, cols].bitcast(FP8X4), w1_q[(a, b)][1][:, cols], v[a], v_plane, 4 * a)
-                for a in range(2)])
+        def make_d(s):
+            return product(table_tile(S, F32), [lhs_of(w3_q[s // PACK], s) + (v3, v3_plane, 0)])
 
-        def d_rows(s):
-            b, t = divmod(s, 4)
-            cols = slice(P * t, P * (t + 1))
-            return product("table", 4, [
-                (w3_q[b][0][:, cols].bitcast(FP8X4), w3_q[b][1][:, cols], v3, v3_plane, 0)])
+        def gather_x(s):
+            x = tile_of("x", [P, PICKS], F32, bufs=PACK)
+            nc.vector.tensor_copy(x[:], a_rows[s][:].indirect(pick1[:]))
+            return x
 
-        xs, rs, z_tiles, ds, ts, us = {}, {}, {}, {}, {}, {}
-        HALF = PK // 2
-        AHEAD = 4
-        units = [(s, 0, PK) for s in range(7)] + [(7, 0, HALF), (7, HALF, HALF + HALF // 2), (7, HALF + HALF // 2, PK)]
+        def make_factor(s):
+            factor = tile_of("factor", [P, PICKS], F32, bufs=PACK)
+            nc.scalar.activation(factor[:], x_of[s][:], ACT.Square)
+            nc.scalar.activation(factor[:], factor[:], ACT.Abs_reciprocal_sqrt, bias=1.0)
+            nc.scalar.activation(factor[:], factor[:], ACT.Square)
+            return factor
 
-        def tmp(name, bufs, i):
-            return work.tile([P, units[i][2] - units[i][1]], F32, name=name, tag=name, bufs=bufs, align_bytes=64)
+        def times_b(term, s):
+            nc.vector.tensor_tensor(term[:, s % PACK, :], b_rows[s][:].indirect(pick2[:]), x_of[s][:], ALU.mult)
 
-        def offsets(pick, i):
-            return pick[:, units[i][1] // 16 : units[i][2] // 16]
+        def times_factor(term, s):
+            nc.vector.tensor_tensor(term[:, s % PACK, :], term[:, s % PACK, :], factor_of[s][:], ALU.mult)
 
-        def curve(i):
-            x = tmp("x", AHEAD, i) if i < AHEAD or True else tmp("b_rows", 8, i)
-            nc.vector.tensor_copy(x[:], a_tiles[units[i][0]][:].indirect(offsets(pick1, i)))
-            r = tmp("r", 4, i)
-            nc.scalar.activation(r[:], x[:], ACT.Square)
-            nc.scalar.activation(r[:], r[:], ACT.Abs_reciprocal_sqrt, bias=1.0)
-            nc.scalar.activation(r[:], r[:], ACT.Square)
-            xs[i], rs[i] = x, r
-
-        def bend(i):
-            eng = nc.gpsimd if i < 0 else nc.vector
-            ts[i] = tmp("bend", 2, i)
-            eng.tensor_tensor(ts[i][:], bs[units[i][0]][:].indirect(offsets(pick2, i)), xs[i][:], ALU.mult)
-
-        def scale(i):
-            us[i] = tmp("u", 2, i)
-            nc.vector.tensor_tensor(us[i][:], ts[i][:], rs[i][:], ALU.mult)
-
-        def shift(i):
-            s, lo, hi = units[i]
-            b, t = divmod(s, 4)
-            if t == 0:
-                z_tiles[b] = work.tile([P, 4, PK], F32, name="raw", tag="raw", bufs=6, align_bytes=64)
+        def plus_d(z, term, s, cols):
+            offsets = pick3[:, cols.start // PER_COLUMN : cols.stop // PER_COLUMN]
             nc.vector.tensor_tensor(
-                z_tiles[b][:, t, lo:hi], ds[s][:].indirect(offsets(pick3, i)), us[i][:], ALU.add)
+                z[:, s % PACK, cols], d_rows[s][:].indirect(offsets), term[:, s % PACK, cols], ALU.add
+            )
 
-        def round_z(b, cols, copy):
-            width = cols.stop - cols.start
-            rounded = work.tile([P, 4 * width], BF16, name="z_rounded", tag="z_rounded", bufs=2, align_bytes=64)
+        def round_z(z, cols, copy):
+            rounded = rounded_tile(PACK * (cols.stop - cols.start))
             copy(
-                rounded[:].rearrange("p (c i t) -> p c t i", i=4, t=4),
-                z_tiles[b][:, :, cols].rearrange("p t (c i) -> p c t i", i=4),
+                rounded[:].rearrange("p (c i t) -> p c t i", i=4, t=PACK),
+                z[:, :, cols].rearrange("p t (c i) -> p c t i", i=4),
             )
             return rounded
 
-        def quantise_z(name, rounded):
-            width = rounded.shape[1] // 4
-            codes = keep.tile([P, width], U32, name=name + "_codes", align_bytes=64)
-            plane = keep.tile([P, width], U8, name=name + "_plane", align_bytes=64)
-            nc.vector.quantize_mx(out=codes[:].bitcast(FP8X4), scales=plane[:], in_=rounded[:])
-            return codes, plane
-
-        def final_pass(acc, b, c, codes, plane):
+        def last_pass(acc, g, c, codes, plane):
             cols = slice(P * c, P * (c + 1))
             nc.tensor.matmul_mx(
-                out=acc, lhsT=w4_tiles[b][:, cols].bitcast(FP8X4), lhsT_scale=w4_plane[4 * b : P, cols],
-                rhs=codes.bitcast(FP8X4), rhs_scale=plane, start=(b == 0), stop=(b == 1),
+                out=acc, lhsT=w4_tiles[g][:, cols].bitcast(FP8X4), lhsT_scale=w4_plane[4 * g : P, cols],
+                rhs=codes.bitcast(FP8X4), rhs_scale=plane, start=(g == 0), stop=(g == 1),
             )
 
-        def store(cols, accs, on_scalar):
-            result = work.tile([P, N // P, cols.stop - cols.start], F32, name="raw", tag="raw", bufs=6, align_bytes=64)
-            for c in range(N // P):
+        def finish(cols, copy, on_scalar):
+            width = cols.stop - cols.start
+            accs = []
+            for c in range(OUT_TILES):
+                accs.append(bank_tile()[:, :width])
+                last_pass(accs[c], 0, c, z0_codes[:, cols], z0_plane[:, cols])
+            name = "z1_%d" % cols.start
+            codes, plane = quantise(round_z(z1, cols, copy), name + "_codes", name + "_plane")
+            for c in range(OUT_TILES):
+                last_pass(accs[c], 1, c, codes, plane)
+            result = big_tile([P, OUT_TILES, width])
+            for c in range(OUT_TILES):
                 if c < on_scalar:
                     nc.scalar.activation(result[:, c, :], accs[c], ACT.Copy, scale=gain_tile[:, c : c + 1])
                 else:
@@ -250,62 +232,90 @@ def tile_list_algae_harvest_join_kernel(
                 if c % 2 == 1:
                     nc.sync.dma_start(
                         out=out[P * (c - 1) : P * (c + 1), cols].rearrange("(c p) j -> p c j", p=P),
-                        in_=result[:, c - 1 : c + 1, :])
+                        in_=result[:, c - 1 : c + 1, :],
+                    )
 
-        def finish(i, copy, tag, on_scalar):
-            cols = slice(units[i][1], units[i][2])
-            accs = []
-            for c in range(N // P):
-                acc = psum.tile([P, BANK], F32, name=tag, tag=tag, bufs=4)
-                accs.append(acc[:, : cols.stop - cols.start])
-                final_pass(accs[c], 0, c, z0[0][:, cols], z0[1][:, cols])
-            codes, plane = quantise_z("z1_%d" % i, round_z(1, cols, copy))
-            for c in range(N // P):
-                final_pass(accs[c], 1, c, codes[:], plane[:])
-            store(cols, accs, on_scalar)
+        w2_codes = tile_of("w2_codes", [P, 2 * H], U8)
+        nc.vector.tensor_copy(
+            w2_codes[:].bitcast(U16).rearrange("p (g t m) -> p g m t", g=2, t=PACK),
+            w2_raw[:].bitcast(U16).rearrange("p (g m t) -> p g m t", g=2, t=PACK),
+        )
+        w2_plane = tile_of("w2_plane", [P, H], U8)
+        nc.vector.tensor_copy(
+            w2_plane[:].rearrange("p (g t m) -> p g m t", g=2, t=PACK),
+            w2_plane_raw[:].rearrange("p (g m t) -> p g m t", g=2, t=PACK),
+        )
+        v2 = gather_words("v2", tab2_tile, list2)
+        v2_plane = gather_plane("v2_plane", tab2_plane, list2)
 
-        r00 = round_weight(w1_raw[(0, 0)], E[0])
-        r10 = round_weight(w1_raw[(1, 0)], E[1])
-        bs = [b_rows(s) for s in range(8)]
-        v = [gather_words("v0", tab_tiles[0], list1)]
+        w1_q, w3_q = {}, {}
+        w1_first = rounded_tile(PACK * PASS)
+        gpsimd_copy(*dealt_views(w1_first[:], w1_raw[0, 0]))
+        w1_second = rounded_tile(PACK * PASS)
+        dst, src = dealt_views(w1_second[:], w1_raw[1, 0])
+        gpsimd_copy(dst[:, : P // 2], src[:, : P // 2])
+        nc.scalar.copy(dst[:, P // 2 :], src[:, P // 2 :])
+        b_rows = [make_b(s, tile_of("b_rows", [P, S], F32, bufs=LAST)) for s in range(LAST)]
+        b_rows.append(make_b(LAST, tile_of("w1_shared", [P, S], F32)))
+
         v_plane = gather_plane("v_plane", tab_plane, list1)
-        w1_q[(0, 0)] = quantise("w1_00", r00)
-        v.append(gather_words("v1", tab_tiles[1], list1))
-        w1_q[(1, 0)] = quantise("w1_10", r10)
-        r3 = round_weight(w3_raw[0], E[2])
-        a_tiles = {s: a_rows(s) for s in range(AHEAD)}
-        v3 = gather_words("v3", tab3_tile, list3)
-        for i in range(2):
-            curve(i)
+        v = [gather_words("v0", tab_tile0, list1)]
         v3_plane = gather_plane("v3_plane", tab3_plane, list3)
-        w3_q[0] = quantise("w3_0", r3)
-        ra = round_weight(w1_raw[(0, 1)], E[3])
-        rb = round_weight(w1_raw[(1, 1)], E[4])
-        rc = round_weight(w3_raw[1], E[5])
-        for i in range(2, AHEAD):
-            curve(i)
-        for i in range(2):
-            ds[i] = d_rows(i)
-        bend(0)
-        for i in range(len(units)):
-            if i == 0:
-                w1_q[(0, 1)] = quantise("w1_01", ra)
-            if i == 0:
-                w1_q[(1, 1)] = quantise("w1_11", rb)
-            if i == 0:
-                w3_q[1] = quantise("w3_1", rc)
-            if i + AHEAD < 8:
-                a_tiles[i + AHEAD] = a_rows(i + AHEAD)
-            if i + 2 < 8:
-                ds[i + 2] = d_rows(i + 2)
-            scale(i)
-            if i + AHEAD < len(units):
-                curve(i + AHEAD)
-            if i + 1 < len(units):
-                bend(i + 1)
-            shift(i)
-            if i == 5:
-                z0 = quantise_z("z0", round_z(0, slice(0, PK), nc.scalar.copy))
-        finish(7, nc.scalar.copy, "fin", 4)
-        finish(8, nc.vector.tensor_copy, "acc", 4)
-        finish(9, nc.vector.tensor_copy, "fin", 2)
+        w1_q[0, 0] = quantise(w1_first, "tab3_plane", "w1_00_plane")
+        v.append(gather_words("v1", tab_tile1, list1))
+        w1_q[1, 0] = quantise(w1_second, "w1_10_codes", "w1_10_plane")
+
+        first, second = range(PACK), range(PACK, SLICES)
+        pair = tile_of("term", [P, 2 * PACK * PASS], BF16)
+        gpsimd_copy(*dealt_views(pair[:, : PACK * PASS], w3_raw[0]))
+        gpsimd_copy(*dealt_views(pair[:, PACK * PASS :], w1_raw[0, 1]))
+        a_rows = {s: make_a(s) for s in first}
+        v3 = gather_words("v3", tab3_tile, list3)
+        x_of = {s: gather_x(s) for s in first}
+        factor_of = {s: make_factor(s) for s in first}
+        pair_codes, pair_plane = quantise(pair, "pair_codes", "pair_plane")
+        w3_q[0] = (pair_codes[:, :PASS], pair_plane[:, :PASS])
+        w1_q[0, 1] = (pair_codes[:, PASS:], pair_plane[:, PASS:])
+        term = tile_of("term", [P, PACK, PICKS], F32)
+        for s in first:
+            times_b(term, s)
+        for s in first:
+            times_factor(term, s)
+        z0 = big_tile([P, PACK, PICKS])
+        d_rows = {}
+        for s in first:
+            d_rows[s] = make_d(s)
+            if s == W1_LAST_AFTER:
+                w1_last = rounded_tile(PACK * PASS)
+                nc.scalar.copy(*dealt_views(w1_last[:], w1_raw[1, 1]))
+                w1_q[1, 1] = quantise(w1_last, "w1_11_codes", "w1_11_plane")
+            plus_d(z0, term, s, ALL_PICKS)
+
+        for s in second:
+            a_rows[s] = make_a(s)
+        w3_last = tile_of("term", [P, PACK * PASS], BF16)
+        gpsimd_copy(*dealt_views(w3_last[:], w3_raw[1]))
+        for s in second:
+            x_of[s] = gather_x(s)
+        w3_q[1] = quantise(w3_last, "w3_1_codes", "a_rows%d" % (LAST % PACK))
+        for s in second:
+            factor_of[s] = make_factor(s)
+            if s == Z0_AFTER:
+                z0_codes, z0_plane = quantise(round_z(z0, ALL_PICKS, nc.scalar.copy), "z0_codes", "z0_plane")
+            if s > PACK:
+                d_rows[s - 1] = make_d(s - 1)
+        d_rows[LAST] = make_d(LAST)
+        term = tile_of("term", [P, PACK, PICKS], F32)
+        for s in second:
+            times_b(term, s)
+        z1 = big_tile([P, PACK, PICKS])
+        for s in second:
+            times_factor(term, s)
+            if s > PACK:
+                plus_d(z1, term, s - 1, ALL_PICKS)
+        for cols in PIECES:
+            plus_d(z1, term, LAST, cols)
+
+        finish(PIECES[0], nc.scalar.copy, OUT_TILES)
+        finish(PIECES[1], nc.vector.tensor_copy, OUT_TILES // 2)
+        finish(PIECES[2], nc.vector.tensor_copy, OUT_TILES // 2)

from contextlib import ExitStack

import concourse.mybir as mybir

K, M, H, N, T, S, PICKS = 1024, 512, 1024, 512, 2048, 1024, 512
FLOPS = 2 * (K * H * S + 2 * M * H * S + H * N * PICKS)

F32 = mybir.dt.float32
BF16 = mybir.dt.bfloat16
I32 = mybir.dt.int32
U32 = mybir.dt.uint32
U16 = mybir.dt.uint16
U8 = mybir.dt.uint8
FP8X4 = mybir.dt.float8_e4m3fn_x4
FP4X4 = mybir.dt.float4_e2m1fn_x4
ACT = mybir.ActivationFunctionType
ALU = mybir.AluOpType

P = 128
PACK = 4
PASS = P * PACK
BANK = 512
BANKS = 8
SLICES = H // P
LAST = SLICES - 1
OUT_TILES = N // P
PER_COLUMN = 16
ALL_PICKS = slice(0, PICKS)

PIECES = [slice(0, PICKS // 2), slice(PICKS // 2, 3 * PICKS // 4), slice(3 * PICKS // 4, PICKS)]
W1_LAST_AFTER = 1
Z0_AFTER = 6


def tile_list_algae_harvest_join_kernel(
    tc, tab_words, tab_scales, tab2_words, tab2_scales, tab3_words, tab3_scales, offs, offs2, offs3,
    pos1, pos2, pos3, w1, w2_words, w2_scales, w3, w4_words, w4_scales, gain, out,
):
    nc = tc.nc
    with ExitStack() as ctx:
        pool = ctx.enter_context(tc.tile_pool(name="sbuf", bufs=1))
        psum = ctx.enter_context(tc.psum_pool(name="psum", bufs=1))

        def tile_of(tag, shape, dtype, bufs=1):
            return pool.tile(shape, dtype, name=tag, tag=tag, bufs=bufs, align_bytes=64)

        def big_tile(shape):
            return tile_of("big", shape, F32, bufs=5)

        def table_tile(width, dtype):
            return tile_of("table", [P, width], dtype, bufs=PACK)

        def rounded_tile(width):
            return tile_of("rounded", [P, width], BF16, bufs=3)

        def bank_tile():
            return psum.tile([P, BANK], F32, name="bank", tag="bank", bufs=BANKS)

        def zeroed_plane(name, width):
            plane = tile_of(name, [P, width], U8)
            nc.vector.memset(plane[:].bitcast(I32), 0)
            return plane

        def load_plane(plane, scales):
            passes = scales.shape[0]
            for quadrant in range(4):
                nc.sync.dma_start(
                    out=plane[32 * quadrant : 32 * quadrant + 4 * passes, :].bitcast(I32),
                    in_=scales[:, 4 * quadrant : 4 * quadrant + 4, :].bitcast(I32),
                )

        def load_list(name, src):
            tile = pool.tile(list(src.shape), U16, name=name)
            nc.sync.dma_start(tile[:], src)
            return tile

        def load_words(tile, words):
            nc.sync.dma_start(out=tile[:], in_=words.rearrange("p c i -> p (c i)").bitcast(I32))
            return tile

        def load_weight(raw, w, g, half):
            rows = w[PASS * g : PASS * (g + 1), PASS * half : PASS * (half + 1)]
            nc.sync.dma_start(out=raw[:], in_=rows.rearrange("(p j) c -> p j c", j=PACK))
            return raw

        tab2_plane = zeroed_plane("tab2_plane", T)
        w2_plane_raw = zeroed_plane("w2_plane_raw", H)
        tab_plane = zeroed_plane("tab_plane", T)
        tab3_plane = zeroed_plane("tab3_plane", T)
        w4_plane = zeroed_plane("w4_plane", N)

        block = [P, PACK, PASS]
        w1_raw, w3_raw = {}, {}
        w2_raw = tile_of("w2_raw", [P, 2 * H], U8)
        nc.sync.dma_start(out=w2_raw[:].bitcast(I32), in_=w2_words[0].bitcast(I32))
        list2 = load_list("list2", offs2)
        load_plane(tab2_plane, tab2_scales)
        tab2_tile = load_words(table_tile(T, I32), tab2_words[0])
        load_plane(w2_plane_raw, w2_scales)
        tab_tile0 = load_words(table_tile(T, I32), tab_words[0])
        list1 = load_list("list1", offs)
        load_plane(tab_plane, tab_scales)
        w1_raw[0, 0] = load_weight(big_tile(block), w1, 0, 0)
        list3 = load_list("list3", offs3)
        load_plane(tab3_plane, tab3_scales)
        tab_tile1 = load_words(table_tile(T, I32), tab_words[1])
        w1_raw[1, 0] = load_weight(tile_of("w1_shared", block, F32), w1, 1, 0)
        tab3_tile = load_words(table_tile(T, I32), tab3_words[0])
        pick1 = load_list("pick1", pos1)
        w3_raw[0] = load_weight(big_tile(block), w3, 0, 0)
        w1_raw[0, 1] = load_weight(big_tile(block), w1, 0, 1)
        pick2 = load_list("pick2", pos2)
        pick3 = load_list("pick3", pos3)
        w1_raw[1, 1] = load_weight(big_tile(block), w1, 1, 1)
        w3_raw[1] = load_weight(big_tile(block), w3, 0, 1)
        w4_tiles = [load_words(tile_of("w4_tile%d" % g, [P, N], I32), w4_words[g]) for g in range(2)]
        load_plane(w4_plane, w4_scales)
        gain_tile = pool.tile([P, OUT_TILES], F32, name="gain_tile")
        with nc.allow_non_contiguous_dma(reason="gain[128 c + p] goes to partition p, as the rows of out do"):
            nc.sync.dma_start(out=gain_tile[:], in_=gain.rearrange("(c p) -> p c", p=P))

        def gather_words(name, table, offsets):
            picked = tile_of(name, [P, S], I32)
            nc.vector.tensor_copy(picked[:].bitcast(U32), table[:].bitcast(U32).indirect(offsets[:]))
            return picked

        def gather_plane(name, plane, offsets):
            picked = tile_of(name, [P, S], U8)
            nc.vector.tensor_copy(picked[:], plane[:].indirect(offsets[:]))
            return picked

        def dealt_views(rounded, raw):
            return (
                rounded.rearrange("p (t m j) -> p m t j", t=PACK, j=PACK),
                raw[:].rearrange("p j (m t) -> p m t j", t=PACK),
            )

        def gpsimd_copy(dst, src):
            nc.gpsimd.tensor_scalar(dst, src, 1.0, 0.0, ALU.mult, ALU.add)

        def quantise(rounded, codes_tag, plane_tag):
            width = rounded.shape[1] // PACK
            codes = tile_of(codes_tag, [P, width], U32)
            plane = tile_of(plane_tag, [P, width], U8)
            nc.vector.quantize_mx(out=codes[:].bitcast(FP8X4), scales=plane[:], in_=rounded[:])
            return codes[:], plane[:]

        def product(rows, passes):
            for first_col in range(0, S, BANK):
                cols = slice(first_col, first_col + BANK)
                acc = bank_tile()
                for g, (lhs, lhs_plane, rhs, rhs_plane, first_row) in enumerate(passes):
                    nc.tensor.matmul_mx(
                        out=acc[:], lhsT=lhs, lhsT_scale=lhs_plane,
                        rhs=rhs[:, cols].bitcast(FP8X4), rhs_scale=rhs_plane[first_row:P, cols],
                        start=(g == 0), stop=(g == len(passes) - 1),
                    )
                nc.scalar.copy(rows[:, cols], acc[:])
            return rows

        def lhs_of(quantised, s):
            codes, plane = quantised
            places = slice(P * (s % PACK), P * (s % PACK + 1))
            return codes[:, places].bitcast(FP8X4), plane[:, places]

        def make_a(s):
            rows = tile_of("a_rows%d" % (s % PACK), [P, S], F32)
            return product(rows, [lhs_of(w1_q[g, s // PACK], s) + (v[g], v_plane, 4 * g) for g in range(2)])

        def make_b(s, rows):
            lhs = w2_codes[:, 2 * P * s : 2 * P * (s + 1)].bitcast(FP4X4)
            return product(rows, [(lhs, w2_plane[:, P * s : P * (s + 1)], v2, v2_plane, 0)])

        def make_d(s):
            return product(table_tile(S, F32), [lhs_of(w3_q[s // PACK], s) + (v3, v3_plane, 0)])

        def gather_x(s):
            x = tile_of("x", [P, PICKS], F32, bufs=PACK)
            nc.vector.tensor_copy(x[:], a_rows[s][:].indirect(pick1[:]))
            return x

        def make_factor(s):
            factor = tile_of("factor", [P, PICKS], F32, bufs=PACK)
            nc.scalar.activation(factor[:], x_of[s][:], ACT.Square)
            nc.scalar.activation(factor[:], factor[:], ACT.Abs_reciprocal_sqrt, bias=1.0)
            nc.scalar.activation(factor[:], factor[:], ACT.Square)
            return factor

        def times_b(term, s):
            nc.vector.tensor_tensor(term[:, s % PACK, :], b_rows[s][:].indirect(pick2[:]), x_of[s][:], ALU.mult)

        def times_factor(term, s):
            nc.vector.tensor_tensor(term[:, s % PACK, :], term[:, s % PACK, :], factor_of[s][:], ALU.mult)

        def plus_d(z, term, s, cols):
            offsets = pick3[:, cols.start // PER_COLUMN : cols.stop // PER_COLUMN]
            nc.vector.tensor_tensor(
                z[:, s % PACK, cols], d_rows[s][:].indirect(offsets), term[:, s % PACK, cols], ALU.add
            )

        def round_z(z, cols, copy):
            rounded = rounded_tile(PACK * (cols.stop - cols.start))
            copy(
                rounded[:].rearrange("p (c i t) -> p c t i", i=4, t=PACK),
                z[:, :, cols].rearrange("p t (c i) -> p c t i", i=4),
            )
            return rounded

        def last_pass(acc, g, c, codes, plane):
            cols = slice(P * c, P * (c + 1))
            nc.tensor.matmul_mx(
                out=acc, lhsT=w4_tiles[g][:, cols].bitcast(FP8X4), lhsT_scale=w4_plane[4 * g : P, cols],
                rhs=codes.bitcast(FP8X4), rhs_scale=plane, start=(g == 0), stop=(g == 1),
            )

        def finish(cols, copy, on_scalar):
            width = cols.stop - cols.start
            accs = []
            for c in range(OUT_TILES):
                accs.append(bank_tile()[:, :width])
                last_pass(accs[c], 0, c, z0_codes[:, cols], z0_plane[:, cols])
            name = "z1_%d" % cols.start
            codes, plane = quantise(round_z(z1, cols, copy), name + "_codes", name + "_plane")
            for c in range(OUT_TILES):
                last_pass(accs[c], 1, c, codes, plane)
            result = big_tile([P, OUT_TILES, width])
            for c in range(OUT_TILES):
                if c < on_scalar:
                    nc.scalar.activation(result[:, c, :], accs[c], ACT.Copy, scale=gain_tile[:, c : c + 1])
                else:
                    nc.vector.tensor_scalar(result[:, c, :], accs[c], gain_tile[:, c : c + 1], None, ALU.mult)
                if c % 2 == 1:
                    nc.sync.dma_start(
                        out=out[P * (c - 1) : P * (c + 1), cols].rearrange("(c p) j -> p c j", p=P),
                        in_=result[:, c - 1 : c + 1, :],
                    )

        w2_codes = tile_of("w2_codes", [P, 2 * H], U8)
        nc.vector.tensor_copy(
            w2_codes[:].bitcast(U16).rearrange("p (g t m) -> p g m t", g=2, t=PACK),
            w2_raw[:].bitcast(U16).rearrange("p (g m t) -> p g m t", g=2, t=PACK),
        )
        w2_plane = tile_of("w2_plane", [P, H], U8)
        nc.vector.tensor_copy(
            w2_plane[:].rearrange("p (g t m) -> p g m t", g=2, t=PACK),
            w2_plane_raw[:].rearrange("p (g m t) -> p g m t", g=2, t=PACK),
        )
        v2 = gather_words("v2", tab2_tile, list2)
        v2_plane = gather_plane("v2_plane", tab2_plane, list2)

        w1_q, w3_q = {}, {}
        w1_first = rounded_tile(PACK * PASS)
        gpsimd_copy(*dealt_views(w1_first[:], w1_raw[0, 0]))
        w1_second = rounded_tile(PACK * PASS)
        dst, src = dealt_views(w1_second[:], w1_raw[1, 0])
        gpsimd_copy(dst[:, : P // 2], src[:, : P // 2])
        nc.scalar.copy(dst[:, P // 2 :], src[:, P // 2 :])
        b_rows = [make_b(s, tile_of("b_rows", [P, S], F32, bufs=LAST)) for s in range(LAST)]
        b_rows.append(make_b(LAST, tile_of("w1_shared", [P, S], F32)))

        v_plane = gather_plane("v_plane", tab_plane, list1)
        v = [gather_words("v0", tab_tile0, list1)]
        v3_plane = gather_plane("v3_plane", tab3_plane, list3)
        w1_q[0, 0] = quantise(w1_first, "tab3_plane", "w1_00_plane")
        v.append(gather_words("v1", tab_tile1, list1))
        w1_q[1, 0] = quantise(w1_second, "w1_10_codes", "w1_10_plane")

        first, second = range(PACK), range(PACK, SLICES)
        pair = tile_of("term", [P, 2 * PACK * PASS], BF16)
        gpsimd_copy(*dealt_views(pair[:, : PACK * PASS], w3_raw[0]))
        gpsimd_copy(*dealt_views(pair[:, PACK * PASS :], w1_raw[0, 1]))
        a_rows = {s: make_a(s) for s in first}
        v3 = gather_words("v3", tab3_tile, list3)
        x_of = {s: gather_x(s) for s in first}
        factor_of = {s: make_factor(s) for s in first}
        pair_codes, pair_plane = quantise(pair, "pair_codes", "pair_plane")
        w3_q[0] = (pair_codes[:, :PASS], pair_plane[:, :PASS])
        w1_q[0, 1] = (pair_codes[:, PASS:], pair_plane[:, PASS:])
        term = tile_of("term", [P, PACK, PICKS], F32)
        for s in first:
            times_b(term, s)
        for s in first:
            times_factor(term, s)
        z0 = big_tile([P, PACK, PICKS])
        d_rows = {}
        for s in first:
            d_rows[s] = make_d(s)
            if s == W1_LAST_AFTER:
                w1_last = rounded_tile(PACK * PASS)
                nc.scalar.copy(*dealt_views(w1_last[:], w1_raw[1, 1]))
                w1_q[1, 1] = quantise(w1_last, "w1_11_codes", "w1_11_plane")
            plus_d(z0, term, s, ALL_PICKS)

        for s in second:
            a_rows[s] = make_a(s)
        w3_last = tile_of("term", [P, PACK * PASS], BF16)
        gpsimd_copy(*dealt_views(w3_last[:], w3_raw[1]))
        for s in second:
            x_of[s] = gather_x(s)
        w3_q[1] = quantise(w3_last, "w3_1_codes", "a_rows%d" % (LAST % PACK))
        for s in second:
            factor_of[s] = make_factor(s)
            if s == Z0_AFTER:
                z0_codes, z0_plane = quantise(round_z(z0, ALL_PICKS, nc.scalar.copy), "z0_codes", "z0_plane")
            if s > PACK:
                d_rows[s - 1] = make_d(s - 1)
        d_rows[LAST] = make_d(LAST)
        term = tile_of("term", [P, PACK, PICKS], F32)
        for s in second:
            times_b(term, s)
        z1 = big_tile([P, PACK, PICKS])
        for s in second:
            times_factor(term, s)
            if s > PACK:
                plus_d(z1, term, s - 1, ALL_PICKS)
        for cols in PIECES:
            plus_d(z1, term, LAST, cols)

        finish(PIECES[0], nc.scalar.copy, OUT_TILES)
        finish(PIECES[1], nc.vector.tensor_copy, OUT_TILES // 2)
        finish(PIECES[2], nc.vector.tensor_copy, OUT_TILES // 2)
